import numpy as np
import ml_dtypes


def mxq(x, axis, fmt="e4m3"):
    dtype, down = {"e4m3": (ml_dtypes.float8_e4m3fn, 7), "e5m2": (ml_dtypes.float8_e5m2, 14)}[fmt]
    v = np.moveaxis(np.asarray(x, np.float32).astype(ml_dtypes.bfloat16).astype(np.float64), axis, -1)
    blocks = v.reshape(v.shape[:-1] + (-1, 32))
    amax = np.abs(blocks).max(-1, keepdims=True)
    byte = np.maximum(np.where(amax > 0, np.frexp(amax)[1] - 1 + 127, 0) - down, 1)
    scale = np.exp2(byte - 127.0)
    codes = (blocks / scale).astype(np.float32).astype(dtype).astype(np.float64)
    return np.moveaxis((codes * scale).reshape(v.shape), -1, axis)


WIDE = False


def mx_kscale(k):
    if not WIDE:
        return np.ones(k)
    levels = np.array([30, -30])
    if k % 512:
        return np.exp2(np.random.permutation(np.resize(levels, k // 32))).repeat(32)
    a = np.empty((k // 512, 16))
    for p in range(k // 512):
        a[p, :8] = np.random.permutation(np.resize(levels, 8))
        for g in range(8):
            far = levels[np.abs(levels - a[p, g]) >= 10]
            a[p, g + 8] = far[np.random.randint(len(far))]
    return np.exp2(a.ravel()).repeat(32)


def f64(x):
    return np.asarray(x).astype(np.float64)


def striped(idx):
    return np.tile(np.asarray(idx).reshape(-1, 16).T, (8, 1)).astype(np.uint16)


def unstriped(offs):
    return offs[:16].T.reshape(-1).astype(np.int64)


E2M1 = np.array([0.0, 0.5, 1.0, 1.5, 2.0, 3.0, 4.0, 6.0, -0.0, -0.5, -1.0, -1.5, -2.0, -3.0, -4.0, -6.0])


def pack_weight(w, fmt):
    k, n = w.shape
    w = f64(np.asarray(w, np.float32).astype(ml_dtypes.bfloat16)).reshape(k // 32, 32, n)
    amax = np.abs(w).max(1)
    if fmt in ("e4m3", "e5m2"):
        byte = np.frexp(amax)[1] - 1 + 127 - (7 if fmt == "e4m3" else 14)
    else:
        mant, ex = np.frexp(amax / 6.0)
        byte = np.where(mant > 0.5, ex, ex - 1) + 127
    byte = np.clip(np.where(amax > 0, byte, 1), 1, 254)
    scaled = (w * np.exp2(127.0 - byte)[:, None, :]).reshape(k, n).astype(np.float32)
    by_word = np.ascontiguousarray(scaled.reshape(k // 512, 128, 4, n).transpose(0, 1, 3, 2))
    if fmt in ("e4m3", "e5m2"):
        words = by_word.astype(ml_dtypes.float8_e4m3fn if fmt == "e4m3" else ml_dtypes.float8_e5m2).view(np.uint8)
    else:
        c = by_word.astype(ml_dtypes.float4_e2m1fn).view(np.uint8) & 0xF
        words = (c[..., 0::2] | (c[..., 1::2] << 4)).reshape(k // 512, 128, 2 * n)
    return np.ascontiguousarray(words), np.ascontiguousarray(byte.astype(np.uint8).reshape(k // 512, 16, n))


def unpack_weight(words, scales, fmt):
    g, _, n = scales.shape
    words = np.ascontiguousarray(words).reshape(g, 128, n, -1)
    if fmt in ("e4m3", "e5m2"):
        vals = words.view(ml_dtypes.float8_e4m3fn if fmt == "e4m3" else ml_dtypes.float8_e5m2).astype(np.float64)
    else:
        nib = np.empty((g, 128, n, 4), np.uint8)
        nib[..., 0::2] = words & 0xF
        nib[..., 1::2] = words >> 4
        vals = E2M1[nib]
    vals = vals * np.repeat(np.exp2(scales.astype(np.float64) - 127.0), 8, axis=1)[..., None]
    return vals.transpose(0, 1, 3, 2).reshape(g * 512, n)


K, T, J, I, R, V = 512, 512, 256, 256, 512, 512


def setup_inputs():
    n = np.random.standard_normal
    idx = np.random.permutation(T)[:J]
    idx2 = np.random.permutation(V)[:J]
    idx3 = np.random.permutation(T)[:I]
    fk = mx_kscale(K)
    fr = mx_kscale(R)
    xtp = pack_weight(n((K, T)) / fk[:, None], "e4m3")
    wap = pack_weight(n((K, R)) * 0.5 / np.sqrt(K) * fk[:, None] * fr, "e5m2")
    wbp = pack_weight(n((K, R)) * 1 / np.sqrt(K) * fk[:, None] / fr, "e2m1")
    return {
        "xt_words": xtp[0],
        "xt_scales": xtp[1],
        "wa_words": wap[0],
        "wa_scales": wap[1],
        "tb": (n((R, V)) * 0.5 * fr[:, None]).astype(np.float32),
        "wb_words": wbp[0],
        "wb_scales": wbp[1],
        "bi": (np.random.uniform(-15.0, 15.0, (1, I))).astype(np.float32),
        "offs": striped(idx),
        "offs2": striped(idx2),
        "offs3": striped(idx3),
    }


def reference(xt_words, xt_scales, wa_words, wa_scales, tb, wb_words, wb_scales, bi, offs, offs2, offs3):
    idx = unstriped(offs)
    idx2 = unstriped(offs2)
    idx3 = unstriped(offs3)
    xtu = unpack_weight(xt_words, xt_scales, "e4m3")
    wau = unpack_weight(wa_words, wa_scales, "e5m2")
    wbu = unpack_weight(wb_words, wb_scales, "e2m1")
    xtidxg = xtu[:, idx]
    za = wau.T @ xtidxg
    ha = np.maximum(za - f64(tb)[:, idx2], 0.0)
    xtidx3g = xtu[:, idx3]
    zb = wbu.T @ xtidx3g
    hb = np.maximum(zb, 0.0)
    haq = mxq(ha, 0, "e4m3")
    hbq = mxq(hb, 0, "e5m2")
    a0 = haq.T @ hbq
    a = a0 + f64(bi)
    mn = np.mean(a, axis=1, keepdims=True)
    d = a - mn
    y = d / (np.mean(np.abs(d), axis=1, keepdims=True) + 4.0)
    return y

@@ -1,0 +1,190 @@
+from contextlib import ExitStack
+
+import concourse.mybir as mybir
+
+K, T, J, I, R, V = 512, 512, 256, 256, 512, 512
+FLOPS = 2 * K * R * J + 2 * K * R * I + 2 * R * J * I
+
+F32 = mybir.dt.float32
+BF16 = mybir.dt.bfloat16
+I32 = mybir.dt.int32
+U32 = mybir.dt.uint32
+U16 = mybir.dt.uint16
+U8 = mybir.dt.uint8
+E4M3 = mybir.dt.float8_e4m3fn_x4
+E5M2 = mybir.dt.float8_e5m2_x4
+E2M1 = mybir.dt.float4_e2m1fn_x4
+ALU = mybir.AluOpType
+ACT = mybir.ActivationFunctionType
+
+P = 128
+PACK = 4
+GROUPS = 16
+HALF = 128
+
+
+def load_scales(queue, plane, scales, q):
+    rows = scales[0].bitcast(I32)[4 * q : 4 * q + 4, :].rearrange("r c -> (r c)")
+    queue.dma_start(out=plane[32 * q : 32 * (q + 1), :].bitcast(I32), in_=rows.partition_broadcast(8))
+
+
+def deal_columns(engine, dealt, raw):
+    engine.tensor_copy(
+        out=dealt[:].bitcast(I32).rearrange("p (t g w) -> p t g w", t=PACK, g=GROUPS),
+        in_=raw[:].bitcast(I32).rearrange("p (g t w) -> p t g w", t=PACK, g=GROUPS),
+    )
+
+
+def tile_list_meet_overtable_plain_spread_kernel(
+    tc, xt_words, xt_scales, wa_words, wa_scales, tb, wb_words, wb_scales, bi, offs, offs2, offs3, out
+):
+    nc = tc.nc
+    with ExitStack() as ctx:
+        keep = ctx.enter_context(tc.tile_pool(name="keep", bufs=1))
+        psum = ctx.enter_context(tc.psum_pool(name="psum", bufs=1))
+
+        list_j = keep.tile([P, J // 16], U16, name="list_j")
+        list_v = keep.tile([P, J // 16], U16, name="list_v")
+        list_i = keep.tile([P, I // 16], U16, name="list_i")
+        xt_w = keep.tile([P, T], U32, name="xt_w", align_bytes=64)
+        xt_s = keep.tile([P, T], U8, name="xt_s", align_bytes=64)
+        wa_raw = keep.tile([P, R], U32, name="wa_raw", align_bytes=64)
+        wa_s_raw = keep.tile([P, R], U8, name="wa_s_raw", align_bytes=64)
+        wb_raw = keep.tile([P, 2 * R], U8, name="wb_raw", align_bytes=64)
+        wb_s_raw = keep.tile([P, R], U8, name="wb_s_raw", align_bytes=64)
+        tb_t = [keep.tile([P, V], F32, name="tb_%d" % t, align_bytes=64) for t in range(PACK)]
+        bias = keep.tile([P, I], F32, name="bias", align_bytes=64)
+
+        tb_rows = tb.rearrange("(g t i) v -> t g i v", t=PACK, g=GROUPS)
+
+        def load_tb(queue, t):
+            queue.dma_start(out=tb_t[t][:], in_=tb_rows[t])
+
+        nc.sync.dma_start(list_j[:], offs)
+        load_scales(nc.scalar, xt_s, xt_scales, 0)
+        load_scales(nc.sync, xt_s, xt_scales, 1)
+        load_scales(nc.scalar, xt_s, xt_scales, 2)
+        load_scales(nc.sync, xt_s, xt_scales, 3)
+        nc.scalar.dma_start(out=xt_w[:].bitcast(I32), in_=xt_words[0].rearrange("p n t -> p (n t)").bitcast(I32))
+        nc.sync.dma_start(out=wa_raw[:].bitcast(I32), in_=wa_words[0].rearrange("p n t -> p (n t)").bitcast(I32))
+        load_tb(nc.scalar, 0)
+        for q in range(4):
+            load_scales(nc.sync, wa_s_raw, wa_scales, q)
+        nc.sync.dma_start(list_i[:], offs3)
+        nc.sync.dma_start(list_v[:], offs2)
+        load_tb(nc.sync, 1)
+        load_tb(nc.sync, 2)
+        nc.sync.dma_start(out=wb_raw[:].bitcast(I32), in_=wb_words[0].bitcast(I32))
+        for q in range(4):
+            load_scales(nc.sync, wb_s_raw, wb_scales, q)
+        load_tb(nc.sync, 3)
+        nc.sync.dma_start(out=bias[:], in_=bi[0].partition_broadcast(P))
+
+        xj_w = keep.tile([P, J], U32, name="xj_w", align_bytes=64)
+        xj_s = keep.tile([P, J], U8, name="xj_s", align_bytes=64)
+        xi_w = keep.tile([P, I], U32, name="xi_w", align_bytes=64)
+        xi_s = keep.tile([P, I], U8, name="xi_s", align_bytes=64)
+        wa_w = keep.tile([P, R], U32, name="wa_w", align_bytes=64)
+        wa_s = keep.tile([P, R], U8, name="wa_s", align_bytes=64)
+        wb_w = keep.tile([P, 2 * R], U8, name="wb_w", align_bytes=64)
+        wb_s = keep.tile([P, R], U8, name="wb_s", align_bytes=64)
+
+        nc.vector.tensor_copy(xj_s[:], xt_s[:].indirect(list_j[:]))
+        nc.vector.tensor_copy(xj_w[:], xt_w[:].indirect(list_j[:]))
+        deal_columns(nc.gpsimd, wa_w, wa_raw)
+        deal_columns(nc.vector, wa_s, wa_s_raw)
+
+        za = [psum.tile([P, 2, J], F32, name="za_%d" % u) for u in range(2)]
+        for t in range(PACK):
+            nc.tensor.matmul_mx(
+                out=za[t // 2][:, t % 2, :],
+                lhsT=wa_w[:, P * t : P * (t + 1)].bitcast(E5M2),
+                lhsT_scale=wa_s[:, P * t : P * (t + 1)],
+                rhs=xj_w[:].bitcast(E4M3),
+                rhs_scale=xj_s[:],
+                start=True,
+                stop=True,
+            )
+
+        nc.vector.tensor_copy(xi_s[:], xt_s[:].indirect(list_i[:]))
+        nc.vector.tensor_copy(xi_w[:], xt_w[:].indirect(list_i[:]))
+        deal_columns(nc.gpsimd, wb_w, wb_raw)
+        deal_columns(nc.vector, wb_s, wb_s_raw)
+
+        zb = [psum.tile([P, PACK, HALF], F32, name="zb_%d" % h) for h in range(2)]
+        for h in range(2):
+            cols = slice(HALF * h, HALF * (h + 1))
+            for t in range(PACK):
+                nc.tensor.matmul_mx(
+                    out=zb[h][:, t, :],
+                    lhsT=wb_w[:, 2 * P * t : 2 * P * (t + 1)].bitcast(E2M1),
+                    lhsT_scale=wb_s[:, P * t : P * (t + 1)],
+                    rhs=xi_w[:, cols].bitcast(E4M3),
+                    rhs_scale=xi_s[:, cols],
+                    start=True,
+                    stop=True,
+                )
+
+        picked = [keep.tile([P, 2, J], F32, name="picked_%d" % u, align_bytes=64) for u in range(2)]
+        for t in range(PACK):
+            nc.scalar.activation(picked[t // 2][:, t % 2, :], tb_t[t][:].indirect(list_v[:]), ACT.Copy)
+
+        diff = keep.tile([P, PACK, J], F32, name="diff", align_bytes=64)
+        nc.vector.tensor_tensor(diff[:, :2, :], za[0][:], picked[0][:], ALU.subtract)
+        for e in range(2):
+            nc.vector.tensor_tensor(diff[:, 2 + e, :], za[1][:, e, :], picked[1][:, e, :], ALU.subtract)
+
+        hb = keep.tile([P, I, PACK], BF16, name="hb", align_bytes=64)
+        for h in range(2):
+            nc.scalar.activation(
+                hb[:, HALF * h : HALF * (h + 1), :], zb[h][:].rearrange("p t n -> p n t"), ACT.Relu
+            )
+        hb_w = keep.tile([P, I], U32, name="hb_w", align_bytes=64)
+        hb_s = keep.tile([P, I], U8, name="hb_s", align_bytes=64)
+
+        ha = [keep.tile([P, HALF, PACK], BF16, name="ha_%d" % h, align_bytes=64) for h in range(2)]
+        nc.vector.tensor_scalar(ha[0][:], diff[:, :, :HALF].rearrange("p t n -> p n t"), 0.0, None, ALU.max)
+        nc.vector.tensor_scalar(ha[1][:], diff[:, :, HALF:].rearrange("p t n -> p n t"), 0.0, None, ALU.max)
+        for h in range(2):
+            cols = slice(HALF * h, HALF * (h + 1))
+            nc.vector.quantize_mx(
+                out=hb_w[:, cols].bitcast(E5M2), scales=hb_s[:, cols], in_=hb[:, cols, :].rearrange("p n t -> p (n t)")
+            )
+
+        acc = [psum.tile([P, I], F32, name="acc_%d" % h) for h in range(2)]
+        for h in range(2):
+            ha_w = keep.tile([P, HALF], U32, name="ha_w_%d" % h, align_bytes=64)
+            ha_s = keep.tile([P, HALF], U8, name="ha_s_%d" % h, align_bytes=64)
+            nc.vector.quantize_mx(
+                out=ha_w[:].bitcast(E4M3), scales=ha_s[:], in_=ha[h][:].rearrange("p n t -> p (n t)")
+            )
+            nc.tensor.matmul_mx(
+                out=acc[h][:],
+                lhsT=ha_w[:].bitcast(E4M3),
+                lhsT_scale=ha_s[:],
+                rhs=hb_w[:].bitcast(E5M2),
+                rhs_scale=hb_s[:],
+                start=True,
+                stop=True,
+            )
+
+        a = [keep.tile([P, I], F32, name="a_%d" % h) for h in range(2)]
+        total = [keep.tile([P, 1], F32, name="total_%d" % h) for h in range(2)]
+        mean = [keep.tile([P, 1], F32, name="mean_%d" % h) for h in range(2)]
+        spread = [keep.tile([P, 1], F32, name="spread_%d" % h) for h in range(2)]
+        for h in range(2):
+            nc.vector.scalar_tensor_tensor(a[h][:], acc[h][:], 1.0, bias[:], ALU.mult, ALU.add, accum_out=total[h][:])
+        for h in range(2):
+            magnitude = keep.tile([P, I], F32, name="magnitude_%d" % h)
+            nc.scalar.activation(
+                magnitude[:], a[h][:], ACT.Abs, bias=total[h][:], scale=-float(I), accum_out=spread[h][:]
+            )
+            nc.vector.tensor_scalar(mean[h][:], total[h][:], 1.0 / I, None, ALU.mult)
+        for h in range(2):
+            denom = keep.tile([P, 1], F32, name="denom_%d" % h)
+            inverse = keep.tile([P, 1], F32, name="inverse_%d" % h)
+            y = keep.tile([P, I], F32, name="y_%d" % h)
+            nc.vector.tensor_scalar(denom[:], spread[h][:], 1.0 / (I * I), 4.0, ALU.mult, ALU.add)
+            nc.vector.reciprocal(inverse[:], denom[:])
+            nc.vector.tensor_scalar(y[:], a[h][:], mean[h][:], inverse[:], ALU.subtract, ALU.mult)
+            nc.sync.dma_start(out=out[HALF * h : HALF * (h + 1), :], in_=y[:])

@@ -24,8 +24,8 @@ HALF = 128
 
 
 def load_scales(queue, plane, scales, q):
-    rows = scales[0].bitcast(I32)[4 * q : 4 * q + 4, :].rearrange("r c -> (r c)")
-    queue.dma_start(out=plane[32 * q : 32 * (q + 1), :].bitcast(I32), in_=rows.partition_broadcast(8))
+    rows = scales[0].bitcast(I32)[4 * q : 4 * q + 4, :]
+    queue.dma_start(out=plane[32 * q : 32 * q + 4, :].bitcast(I32), in_=rows)
 
 
 def deal_columns(engine, dealt, raw):
@@ -60,18 +60,20 @@ def tile_list_meet_overtable_plain_spread_kernel(
         def load_tb(queue, t):
             queue.dma_start(out=tb_t[t][:], in_=tb_rows[t])
 
+        nc.vector.memset(xt_s[:].bitcast(I32), 0)
+        nc.vector.memset(wa_s_raw[:].bitcast(I32), 0)
+        nc.vector.memset(wb_s_raw[:].bitcast(I32), 0)
+
         nc.sync.dma_start(list_j[:], offs)
-        load_scales(nc.scalar, xt_s, xt_scales, 0)
-        load_scales(nc.sync, xt_s, xt_scales, 1)
-        load_scales(nc.scalar, xt_s, xt_scales, 2)
-        load_scales(nc.sync, xt_s, xt_scales, 3)
-        nc.scalar.dma_start(out=xt_w[:].bitcast(I32), in_=xt_words[0].rearrange("p n t -> p (n t)").bitcast(I32))
+        nc.sync.dma_start(out=xt_w[:].bitcast(I32), in_=xt_words[0].rearrange("p n t -> p (n t)").bitcast(I32))
+        for q in range(4):
+            load_scales(nc.sync, xt_s, xt_scales, q)
+        nc.sync.dma_start(list_v[:], offs2)
+        load_tb(nc.sync, 0)
         nc.sync.dma_start(out=wa_raw[:].bitcast(I32), in_=wa_words[0].rearrange("p n t -> p (n t)").bitcast(I32))
-        load_tb(nc.scalar, 0)
         for q in range(4):
             load_scales(nc.sync, wa_s_raw, wa_scales, q)
         nc.sync.dma_start(list_i[:], offs3)
-        nc.sync.dma_start(list_v[:], offs2)
         load_tb(nc.sync, 1)
         load_tb(nc.sync, 2)
         nc.sync.dma_start(out=wb_raw[:].bitcast(I32), in_=wb_words[0].bitcast(I32))
@@ -89,9 +91,9 @@ def tile_list_meet_overtable_plain_spread_kernel(
         wb_w = keep.tile([P, 2 * R], U8, name="wb_w", align_bytes=64)
         wb_s = keep.tile([P, R], U8, name="wb_s", align_bytes=64)
 
-        nc.vector.tensor_copy(xj_s[:], xt_s[:].indirect(list_j[:]))
         nc.vector.tensor_copy(xj_w[:], xt_w[:].indirect(list_j[:]))
-        deal_columns(nc.gpsimd, wa_w, wa_raw)
+        nc.vector.tensor_copy(xj_s[:], xt_s[:].indirect(list_j[:]))
+        deal_columns(nc.vector, wa_w, wa_raw)
         deal_columns(nc.vector, wa_s, wa_s_raw)
 
         za = [psum.tile([P, 2, J], F32, name="za_%d" % u) for u in range(2)]
@@ -108,7 +110,7 @@ def tile_list_meet_overtable_plain_spread_kernel(
 
         nc.vector.tensor_copy(xi_s[:], xt_s[:].indirect(list_i[:]))
         nc.vector.tensor_copy(xi_w[:], xt_w[:].indirect(list_i[:]))
-        deal_columns(nc.gpsimd, wb_w, wb_raw)
+        deal_columns(nc.vector, wb_w, wb_raw)
         deal_columns(nc.vector, wb_s, wb_s_raw)
 
         zb = [psum.tile([P, PACK, HALF], F32, name="zb_%d" % h) for h in range(2)]
@@ -145,6 +147,12 @@ def tile_list_meet_overtable_plain_spread_kernel(
         ha = [keep.tile([P, HALF, PACK], BF16, name="ha_%d" % h, align_bytes=64) for h in range(2)]
         nc.vector.tensor_scalar(ha[0][:], diff[:, :, :HALF].rearrange("p t n -> p n t"), 0.0, None, ALU.max)
         nc.vector.tensor_scalar(ha[1][:], diff[:, :, HALF:].rearrange("p t n -> p n t"), 0.0, None, ALU.max)
+        ha_w = [keep.tile([P, HALF], U32, name="ha_w_%d" % h, align_bytes=64) for h in range(2)]
+        ha_s = [keep.tile([P, HALF], U8, name="ha_s_%d" % h, align_bytes=64) for h in range(2)]
+        for h in range(2):
+            nc.vector.quantize_mx(
+                out=ha_w[h][:].bitcast(E4M3), scales=ha_s[h][:], in_=ha[h][:].rearrange("p n t -> p (n t)")
+            )
         for h in range(2):
             cols = slice(HALF * h, HALF * (h + 1))
             nc.vector.quantize_mx(
@@ -152,39 +160,34 @@ def tile_list_meet_overtable_plain_spread_kernel(
             )
 
         acc = [psum.tile([P, I], F32, name="acc_%d" % h) for h in range(2)]
-        for h in range(2):
-            ha_w = keep.tile([P, HALF], U32, name="ha_w_%d" % h, align_bytes=64)
-            ha_s = keep.tile([P, HALF], U8, name="ha_s_%d" % h, align_bytes=64)
-            nc.vector.quantize_mx(
-                out=ha_w[:].bitcast(E4M3), scales=ha_s[:], in_=ha[h][:].rearrange("p n t -> p (n t)")
-            )
-            nc.tensor.matmul_mx(
-                out=acc[h][:],
-                lhsT=ha_w[:].bitcast(E4M3),
-                lhsT_scale=ha_s[:],
-                rhs=hb_w[:].bitcast(E5M2),
-                rhs_scale=hb_s[:],
-                start=True,
-                stop=True,
-            )
+        for c in range(2):
+            cols = slice(HALF * c, HALF * (c + 1))
+            for h in range(2):
+                nc.tensor.matmul_mx(
+                    out=acc[h][:, cols],
+                    lhsT=ha_w[h][:].bitcast(E4M3),
+                    lhsT_scale=ha_s[h][:],
+                    rhs=hb_w[:, cols].bitcast(E5M2),
+                    rhs_scale=hb_s[:, cols],
+                    start=True,
+                    stop=True,
+                )
 
         a = [keep.tile([P, I], F32, name="a_%d" % h) for h in range(2)]
         total = [keep.tile([P, 1], F32, name="total_%d" % h) for h in range(2)]
-        mean = [keep.tile([P, 1], F32, name="mean_%d" % h) for h in range(2)]
-        spread = [keep.tile([P, 1], F32, name="spread_%d" % h) for h in range(2)]
+        root = [keep.tile([P, 1], F32, name="root_%d" % h) for h in range(2)]
+        centred = [keep.tile([P, I], F32, name="centred_%d" % h) for h in range(2)]
         for h in range(2):
             nc.vector.scalar_tensor_tensor(a[h][:], acc[h][:], 1.0, bias[:], ALU.mult, ALU.add, accum_out=total[h][:])
         for h in range(2):
             magnitude = keep.tile([P, I], F32, name="magnitude_%d" % h)
+            spread = keep.tile([P, 1], F32, name="spread_%d" % h)
             nc.scalar.activation(
-                magnitude[:], a[h][:], ACT.Abs, bias=total[h][:], scale=-float(I), accum_out=spread[h][:]
+                magnitude[:], a[h][:], ACT.Abs, bias=total[h][:], scale=-float(I), accum_out=spread[:]
             )
-            nc.vector.tensor_scalar(mean[h][:], total[h][:], 1.0 / I, None, ALU.mult)
+            nc.scalar.activation(root[h][:], spread[:], ACT.Abs_reciprocal_sqrt, bias=4.0 * I, scale=1.0 / I)
+            nc.vector.tensor_scalar(centred[h][:], a[h][:], float(I), total[h][:], ALU.mult, ALU.subtract)
         for h in range(2):
-            denom = keep.tile([P, 1], F32, name="denom_%d" % h)
-            inverse = keep.tile([P, 1], F32, name="inverse_%d" % h)
             y = keep.tile([P, I], F32, name="y_%d" % h)
-            nc.vector.tensor_scalar(denom[:], spread[h][:], 1.0 / (I * I), 4.0, ALU.mult, ALU.add)
-            nc.vector.reciprocal(inverse[:], denom[:])
-            nc.vector.tensor_scalar(y[:], a[h][:], mean[h][:], inverse[:], ALU.subtract, ALU.mult)
+            nc.vector.tensor_scalar(y[:], centred[h][:], root[h][:], root[h][:], ALU.mult, ALU.mult)
             nc.sync.dma_start(out=out[HALF * h : HALF * (h + 1), :], in_=y[:])

@@ -82,6 +82,11 @@ def tile_list_meet_overtable_plain_spread_kernel(
         load_tb(nc.sync, 3)
         nc.sync.dma_start(out=bias[:], in_=bi[0].partition_broadcast(P))
 
+        warm_in = keep.tile([P, 1], F32, name="warm_in")
+        warm_out = keep.tile([P, 1], F32, name="warm_out")
+        nc.vector.memset(warm_in[:], 0.0)
+        nc.scalar.activation(warm_out[:], warm_in[:], ACT.Abs_reciprocal_sqrt, bias=4.0 * I)
+
         xj_w = keep.tile([P, J], U32, name="xj_w", align_bytes=64)
         xj_s = keep.tile([P, J], U8, name="xj_s", align_bytes=64)
         xi_w = keep.tile([P, I], U32, name="xi_w", align_bytes=64)

@@ -24,6 +24,11 @@ HALF = 128
 
 
 def load_scales(queue, plane, scales, q):
+    rows = scales[0].bitcast(I32)[4 * q : 4 * q + 4, :].rearrange("r c -> (r c)")
+    queue.dma_start(out=plane[32 * q : 32 * (q + 1), :].bitcast(I32), in_=rows.partition_broadcast(8))
+
+
+def load_live_rows(queue, plane, scales, q):
     rows = scales[0].bitcast(I32)[4 * q : 4 * q + 4, :]
     queue.dma_start(out=plane[32 * q : 32 * q + 4, :].bitcast(I32), in_=rows)
 
@@ -60,25 +65,29 @@ def tile_list_meet_overtable_plain_spread_kernel(
         def load_tb(queue, t):
             queue.dma_start(out=tb_t[t][:], in_=tb_rows[t])
 
-        nc.vector.memset(xt_s[:].bitcast(I32), 0)
-        nc.vector.memset(wa_s_raw[:].bitcast(I32), 0)
         nc.vector.memset(wb_s_raw[:].bitcast(I32), 0)
 
         nc.sync.dma_start(list_j[:], offs)
-        nc.sync.dma_start(out=xt_w[:].bitcast(I32), in_=xt_words[0].rearrange("p n t -> p (n t)").bitcast(I32))
-        for q in range(4):
-            load_scales(nc.sync, xt_s, xt_scales, q)
-        nc.sync.dma_start(list_v[:], offs2)
-        load_tb(nc.sync, 0)
+        load_scales(nc.scalar, xt_s, xt_scales, 0)
+        load_scales(nc.sync, xt_s, xt_scales, 1)
+        load_scales(nc.scalar, xt_s, xt_scales, 2)
+        load_scales(nc.sync, xt_s, xt_scales, 3)
+        nc.scalar.dma_start(out=xt_w[:].bitcast(I32), in_=xt_words[0].rearrange("p n t -> p (n t)").bitcast(I32))
         nc.sync.dma_start(out=wa_raw[:].bitcast(I32), in_=wa_words[0].rearrange("p n t -> p (n t)").bitcast(I32))
-        for q in range(4):
-            load_scales(nc.sync, wa_s_raw, wa_scales, q)
+        load_tb(nc.scalar, 0)
+        load_scales(nc.gpsimd, wa_s_raw, wa_scales, 0)
+        load_scales(nc.gpsimd, wa_s_raw, wa_scales, 1)
+        load_scales(nc.sync, wa_s_raw, wa_scales, 2)
+        load_scales(nc.sync, wa_s_raw, wa_scales, 3)
         nc.sync.dma_start(list_i[:], offs3)
+        nc.sync.dma_start(list_v[:], offs2)
         load_tb(nc.sync, 1)
         load_tb(nc.sync, 2)
         nc.sync.dma_start(out=wb_raw[:].bitcast(I32), in_=wb_words[0].bitcast(I32))
-        for q in range(4):
-            load_scales(nc.sync, wb_s_raw, wb_scales, q)
+        load_live_rows(nc.sync, wb_s_raw, wb_scales, 0)
+        load_live_rows(nc.sync, wb_s_raw, wb_scales, 1)
+        load_live_rows(nc.sync, wb_s_raw, wb_scales, 2)
+        load_live_rows(nc.sync, wb_s_raw, wb_scales, 3)
         load_tb(nc.sync, 3)
         nc.sync.dma_start(out=bias[:], in_=bi[0].partition_broadcast(P))
 
@@ -96,8 +105,8 @@ def tile_list_meet_overtable_plain_spread_kernel(
         wb_w = keep.tile([P, 2 * R], U8, name="wb_w", align_bytes=64)
         wb_s = keep.tile([P, R], U8, name="wb_s", align_bytes=64)
 
-        nc.vector.tensor_copy(xj_w[:], xt_w[:].indirect(list_j[:]))
         nc.vector.tensor_copy(xj_s[:], xt_s[:].indirect(list_j[:]))
+        nc.vector.tensor_copy(xj_w[:], xt_w[:].indirect(list_j[:]))
         deal_columns(nc.vector, wa_w, wa_raw)
         deal_columns(nc.vector, wa_s, wa_s_raw)
 
@@ -115,8 +124,8 @@ def tile_list_meet_overtable_plain_spread_kernel(
 
         nc.vector.tensor_copy(xi_s[:], xt_s[:].indirect(list_i[:]))
         nc.vector.tensor_copy(xi_w[:], xt_w[:].indirect(list_i[:]))
-        deal_columns(nc.vector, wb_w, wb_raw)
-        deal_columns(nc.vector, wb_s, wb_s_raw)
+        deal_columns(nc.gpsimd, wb_w, wb_raw)
+        deal_columns(nc.gpsimd, wb_s, wb_s_raw)
 
         zb = [psum.tile([P, PACK, HALF], F32, name="zb_%d" % h) for h in range(2)]
         for h in range(2):
@@ -133,13 +142,19 @@ def tile_list_meet_overtable_plain_spread_kernel(
                 )
 
         picked = [keep.tile([P, 2, J], F32, name="picked_%d" % u, align_bytes=64) for u in range(2)]
-        for t in range(PACK):
+        for t in range(PACK - 1):
             nc.scalar.activation(picked[t // 2][:, t % 2, :], tb_t[t][:].indirect(list_v[:]), ACT.Copy)
+        for h in range(2):
+            nc.scalar.activation(
+                picked[1][:, 1, HALF * h : HALF * (h + 1)], tb_t[3][:].indirect(list_v[:, 8 * h : 8 * (h + 1)]), ACT.Copy
+            )
 
         diff = keep.tile([P, PACK, J], F32, name="diff", align_bytes=64)
         nc.vector.tensor_tensor(diff[:, :2, :], za[0][:], picked[0][:], ALU.subtract)
-        for e in range(2):
-            nc.vector.tensor_tensor(diff[:, 2 + e, :], za[1][:, e, :], picked[1][:, e, :], ALU.subtract)
+        nc.vector.tensor_tensor(diff[:, 2, :], za[1][:, 0, :], picked[1][:, 0, :], ALU.subtract)
+        for h in range(2):
+            cols = slice(HALF * h, HALF * (h + 1))
+            nc.vector.tensor_tensor(diff[:, 3, cols], za[1][:, 1, cols], picked[1][:, 1, cols], ALU.subtract)
 
         hb = keep.tile([P, I, PACK], BF16, name="hb", align_bytes=64)
         for h in range(2):

@@ -1,6 +1,7 @@
 from contextlib import ExitStack
 
 import concourse.mybir as mybir
+from concourse.masks import make_identity
 
 K, T, J, I, R, V = 512, 512, 256, 256, 512, 512
 FLOPS = 2 * K * R * J + 2 * K * R * I + 2 * R * J * I
@@ -59,6 +60,8 @@ def tile_list_meet_overtable_plain_spread_kernel(
         wb_s_raw = keep.tile([P, R], U8, name="wb_s_raw", align_bytes=64)
         tb_t = [keep.tile([P, V], F32, name="tb_%d" % t, align_bytes=64) for t in range(PACK)]
         bias = keep.tile([P, I], F32, name="bias", align_bytes=64)
+        bias_pairs = keep.tile([P, 2], F32, name="bias_pairs", align_bytes=64)
+        identity = keep.tile([P, P], F32, name="identity", align_bytes=64)
 
         tb_rows = tb.rearrange("(g t i) v -> t g i v", t=PACK, g=GROUPS)
 
@@ -89,7 +92,8 @@ def tile_list_meet_overtable_plain_spread_kernel(
         load_live_rows(nc.sync, wb_s_raw, wb_scales, 2)
         load_live_rows(nc.sync, wb_s_raw, wb_scales, 3)
         load_tb(nc.sync, 3)
-        nc.sync.dma_start(out=bias[:], in_=bi[0].partition_broadcast(P))
+        nc.sync.dma_start(out=bias_pairs[:], in_=bi[0].rearrange("(p e) -> p e", e=2))
+        make_identity(nc, identity[:])
 
         warm_in = keep.tile([P, 1], F32, name="warm_in")
         warm_out = keep.tile([P, 1], F32, name="warm_out")
@@ -161,6 +165,9 @@ def tile_list_meet_overtable_plain_spread_kernel(
             nc.scalar.activation(
                 hb[:, HALF * h : HALF * (h + 1), :], zb[h][:].rearrange("p t n -> p n t"), ACT.Relu
             )
+        for e in range(2):
+            nc.tensor.transpose(zb[0][:, e, :], bias_pairs[:, e : e + 1].to_broadcast([P, P]), identity[:])
+        nc.scalar.copy(bias[:].rearrange("p (n e) -> p n e", e=2), zb[0][:, :2, :].rearrange("p e n -> p n e"))
         hb_w = keep.tile([P, I], U32, name="hb_w", align_bytes=64)
         hb_s = keep.tile([P, I], U8, name="hb_s", align_bytes=64)
 

from contextlib import ExitStack

import concourse.mybir as mybir
from concourse.masks import make_identity

K, T, J, I, R, V = 512, 512, 256, 256, 512, 512
FLOPS = 2 * K * R * J + 2 * K * R * I + 2 * R * J * I

F32 = mybir.dt.float32
BF16 = mybir.dt.bfloat16
I32 = mybir.dt.int32
U32 = mybir.dt.uint32
U16 = mybir.dt.uint16
U8 = mybir.dt.uint8
E4M3 = mybir.dt.float8_e4m3fn_x4
E5M2 = mybir.dt.float8_e5m2_x4
E2M1 = mybir.dt.float4_e2m1fn_x4
ALU = mybir.AluOpType
ACT = mybir.ActivationFunctionType

P = 128
PACK = 4
GROUPS = 16
HALF = 128


def load_scales(queue, plane, scales, q):
    rows = scales[0].bitcast(I32)[4 * q : 4 * q + 4, :].rearrange("r c -> (r c)")
    queue.dma_start(out=plane[32 * q : 32 * (q + 1), :].bitcast(I32), in_=rows.partition_broadcast(8))


def load_live_rows(queue, plane, scales, q):
    rows = scales[0].bitcast(I32)[4 * q : 4 * q + 4, :]
    queue.dma_start(out=plane[32 * q : 32 * q + 4, :].bitcast(I32), in_=rows)


def deal_columns(engine, dealt, raw):
    engine.tensor_copy(
        out=dealt[:].bitcast(I32).rearrange("p (t g w) -> p t g w", t=PACK, g=GROUPS),
        in_=raw[:].bitcast(I32).rearrange("p (g t w) -> p t g w", t=PACK, g=GROUPS),
    )


def tile_list_meet_overtable_plain_spread_kernel(
    tc, xt_words, xt_scales, wa_words, wa_scales, tb, wb_words, wb_scales, bi, offs, offs2, offs3, out
):
    nc = tc.nc
    with ExitStack() as ctx:
        keep = ctx.enter_context(tc.tile_pool(name="keep", bufs=1))
        psum = ctx.enter_context(tc.psum_pool(name="psum", bufs=1))

        list_j = keep.tile([P, J // 16], U16, name="list_j")
        list_v = keep.tile([P, J // 16], U16, name="list_v")
        list_i = keep.tile([P, I // 16], U16, name="list_i")
        xt_w = keep.tile([P, T], U32, name="xt_w", align_bytes=64)
        xt_s = keep.tile([P, T], U8, name="xt_s", align_bytes=64)
        wa_raw = keep.tile([P, R], U32, name="wa_raw", align_bytes=64)
        wa_s_raw = keep.tile([P, R], U8, name="wa_s_raw", align_bytes=64)
        wb_raw = keep.tile([P, 2 * R], U8, name="wb_raw", align_bytes=64)
        wb_s_raw = keep.tile([P, R], U8, name="wb_s_raw", align_bytes=64)
        tb_t = [keep.tile([P, V], F32, name="tb_%d" % t, align_bytes=64) for t in range(PACK)]
        bias = keep.tile([P, I], F32, name="bias", align_bytes=64)
        bias_pairs = keep.tile([P, 2], F32, name="bias_pairs", align_bytes=64)
        identity = keep.tile([P, P], F32, name="identity", align_bytes=64)

        tb_rows = tb.rearrange("(g t i) v -> t g i v", t=PACK, g=GROUPS)

        def load_tb(queue, t):
            queue.dma_start(out=tb_t[t][:], in_=tb_rows[t])

        nc.vector.memset(wb_s_raw[:].bitcast(I32), 0)

        nc.sync.dma_start(list_j[:], offs)
        load_scales(nc.scalar, xt_s, xt_scales, 0)
        load_scales(nc.sync, xt_s, xt_scales, 1)
        load_scales(nc.scalar, xt_s, xt_scales, 2)
        load_scales(nc.sync, xt_s, xt_scales, 3)
        nc.scalar.dma_start(out=xt_w[:].bitcast(I32), in_=xt_words[0].rearrange("p n t -> p (n t)").bitcast(I32))
        nc.sync.dma_start(out=wa_raw[:].bitcast(I32), in_=wa_words[0].rearrange("p n t -> p (n t)").bitcast(I32))
        load_tb(nc.scalar, 0)
        load_scales(nc.gpsimd, wa_s_raw, wa_scales, 0)
        load_scales(nc.gpsimd, wa_s_raw, wa_scales, 1)
        load_scales(nc.sync, wa_s_raw, wa_scales, 2)
        load_scales(nc.sync, wa_s_raw, wa_scales, 3)
        nc.sync.dma_start(list_i[:], offs3)
        nc.sync.dma_start(list_v[:], offs2)
        load_tb(nc.sync, 1)
        load_tb(nc.sync, 2)
        nc.sync.dma_start(out=wb_raw[:].bitcast(I32), in_=wb_words[0].bitcast(I32))
        load_live_rows(nc.sync, wb_s_raw, wb_scales, 0)
        load_live_rows(nc.sync, wb_s_raw, wb_scales, 1)
        load_live_rows(nc.sync, wb_s_raw, wb_scales, 2)
        load_live_rows(nc.sync, wb_s_raw, wb_scales, 3)
        load_tb(nc.sync, 3)
        nc.sync.dma_start(out=bias_pairs[:], in_=bi[0].rearrange("(p e) -> p e", e=2))
        make_identity(nc, identity[:])

        warm_in = keep.tile([P, 1], F32, name="warm_in")
        warm_out = keep.tile([P, 1], F32, name="warm_out")
        nc.vector.memset(warm_in[:], 0.0)
        nc.scalar.activation(warm_out[:], warm_in[:], ACT.Abs_reciprocal_sqrt, bias=4.0 * I)

        xj_w = keep.tile([P, J], U32, name="xj_w", align_bytes=64)
        xj_s = keep.tile([P, J], U8, name="xj_s", align_bytes=64)
        xi_w = keep.tile([P, I], U32, name="xi_w", align_bytes=64)
        xi_s = keep.tile([P, I], U8, name="xi_s", align_bytes=64)
        wa_w = keep.tile([P, R], U32, name="wa_w", align_bytes=64)
        wa_s = keep.tile([P, R], U8, name="wa_s", align_bytes=64)
        wb_w = keep.tile([P, 2 * R], U8, name="wb_w", align_bytes=64)
        wb_s = keep.tile([P, R], U8, name="wb_s", align_bytes=64)

        nc.vector.tensor_copy(xj_s[:], xt_s[:].indirect(list_j[:]))
        nc.vector.tensor_copy(xj_w[:], xt_w[:].indirect(list_j[:]))
        deal_columns(nc.vector, wa_w, wa_raw)
        deal_columns(nc.vector, wa_s, wa_s_raw)

        za = [psum.tile([P, 2, J], F32, name="za_%d" % u) for u in range(2)]
        for t in range(PACK):
            nc.tensor.matmul_mx(
                out=za[t // 2][:, t % 2, :],
                lhsT=wa_w[:, P * t : P * (t + 1)].bitcast(E5M2),
                lhsT_scale=wa_s[:, P * t : P * (t + 1)],
                rhs=xj_w[:].bitcast(E4M3),
                rhs_scale=xj_s[:],
                start=True,
                stop=True,
            )

        nc.vector.tensor_copy(xi_s[:], xt_s[:].indirect(list_i[:]))
        nc.vector.tensor_copy(xi_w[:], xt_w[:].indirect(list_i[:]))
        deal_columns(nc.gpsimd, wb_w, wb_raw)
        deal_columns(nc.gpsimd, wb_s, wb_s_raw)

        zb = [psum.tile([P, PACK, HALF], F32, name="zb_%d" % h) for h in range(2)]
        for h in range(2):
            cols = slice(HALF * h, HALF * (h + 1))
            for t in range(PACK):
                nc.tensor.matmul_mx(
                    out=zb[h][:, t, :],
                    lhsT=wb_w[:, 2 * P * t : 2 * P * (t + 1)].bitcast(E2M1),
                    lhsT_scale=wb_s[:, P * t : P * (t + 1)],
                    rhs=xi_w[:, cols].bitcast(E4M3),
                    rhs_scale=xi_s[:, cols],
                    start=True,
                    stop=True,
                )

        picked = [keep.tile([P, 2, J], F32, name="picked_%d" % u, align_bytes=64) for u in range(2)]
        for t in range(PACK - 1):
            nc.scalar.activation(picked[t // 2][:, t % 2, :], tb_t[t][:].indirect(list_v[:]), ACT.Copy)
        for h in range(2):
            nc.scalar.activation(
                picked[1][:, 1, HALF * h : HALF * (h + 1)], tb_t[3][:].indirect(list_v[:, 8 * h : 8 * (h + 1)]), ACT.Copy
            )

        diff = keep.tile([P, PACK, J], F32, name="diff", align_bytes=64)
        nc.vector.tensor_tensor(diff[:, :2, :], za[0][:], picked[0][:], ALU.subtract)
        nc.vector.tensor_tensor(diff[:, 2, :], za[1][:, 0, :], picked[1][:, 0, :], ALU.subtract)
        for h in range(2):
            cols = slice(HALF * h, HALF * (h + 1))
            nc.vector.tensor_tensor(diff[:, 3, cols], za[1][:, 1, cols], picked[1][:, 1, cols], ALU.subtract)

        hb = keep.tile([P, I, PACK], BF16, name="hb", align_bytes=64)
        for h in range(2):
            nc.scalar.activation(
                hb[:, HALF * h : HALF * (h + 1), :], zb[h][:].rearrange("p t n -> p n t"), ACT.Relu
            )
        for e in range(2):
            nc.tensor.transpose(zb[0][:, e, :], bias_pairs[:, e : e + 1].to_broadcast([P, P]), identity[:])
        nc.scalar.copy(bias[:].rearrange("p (n e) -> p n e", e=2), zb[0][:, :2, :].rearrange("p e n -> p n e"))
        hb_w = keep.tile([P, I], U32, name="hb_w", align_bytes=64)
        hb_s = keep.tile([P, I], U8, name="hb_s", align_bytes=64)

        ha = [keep.tile([P, HALF, PACK], BF16, name="ha_%d" % h, align_bytes=64) for h in range(2)]
        nc.vector.tensor_scalar(ha[0][:], diff[:, :, :HALF].rearrange("p t n -> p n t"), 0.0, None, ALU.max)
        nc.vector.tensor_scalar(ha[1][:], diff[:, :, HALF:].rearrange("p t n -> p n t"), 0.0, None, ALU.max)
        ha_w = [keep.tile([P, HALF], U32, name="ha_w_%d" % h, align_bytes=64) for h in range(2)]
        ha_s = [keep.tile([P, HALF], U8, name="ha_s_%d" % h, align_bytes=64) for h in range(2)]
        for h in range(2):
            nc.vector.quantize_mx(
                out=ha_w[h][:].bitcast(E4M3), scales=ha_s[h][:], in_=ha[h][:].rearrange("p n t -> p (n t)")
            )
        for h in range(2):
            cols = slice(HALF * h, HALF * (h + 1))
            nc.vector.quantize_mx(
                out=hb_w[:, cols].bitcast(E5M2), scales=hb_s[:, cols], in_=hb[:, cols, :].rearrange("p n t -> p (n t)")
            )

        acc = [psum.tile([P, I], F32, name="acc_%d" % h) for h in range(2)]
        for c in range(2):
            cols = slice(HALF * c, HALF * (c + 1))
            for h in range(2):
                nc.tensor.matmul_mx(
                    out=acc[h][:, cols],
                    lhsT=ha_w[h][:].bitcast(E4M3),
                    lhsT_scale=ha_s[h][:],
                    rhs=hb_w[:, cols].bitcast(E5M2),
                    rhs_scale=hb_s[:, cols],
                    start=True,
                    stop=True,
                )

        a = [keep.tile([P, I], F32, name="a_%d" % h) for h in range(2)]
        total = [keep.tile([P, 1], F32, name="total_%d" % h) for h in range(2)]
        root = [keep.tile([P, 1], F32, name="root_%d" % h) for h in range(2)]
        centred = [keep.tile([P, I], F32, name="centred_%d" % h) for h in range(2)]
        for h in range(2):
            nc.vector.scalar_tensor_tensor(a[h][:], acc[h][:], 1.0, bias[:], ALU.mult, ALU.add, accum_out=total[h][:])
        for h in range(2):
            magnitude = keep.tile([P, I], F32, name="magnitude_%d" % h)
            spread = keep.tile([P, 1], F32, name="spread_%d" % h)
            nc.scalar.activation(
                magnitude[:], a[h][:], ACT.Abs, bias=total[h][:], scale=-float(I), accum_out=spread[:]
            )
            nc.scalar.activation(root[h][:], spread[:], ACT.Abs_reciprocal_sqrt, bias=4.0 * I, scale=1.0 / I)
            nc.vector.tensor_scalar(centred[h][:], a[h][:], float(I), total[h][:], ALU.mult, ALU.subtract)
        for h in range(2):
            y = keep.tile([P, I], F32, name="y_%d" % h)
            nc.vector.tensor_scalar(y[:], centred[h][:], root[h][:], root[h][:], ALU.mult, ALU.mult)
            nc.sync.dma_start(out=out[HALF * h : HALF * (h + 1), :], in_=y[:])
